import numpy as np
import ml_dtypes


def mxq(x, axis, fmt="e4m3"):
    dtype, down = {"e4m3": (ml_dtypes.float8_e4m3fn, 7), "e5m2": (ml_dtypes.float8_e5m2, 14)}[fmt]
    v = np.moveaxis(np.asarray(x, np.float32).astype(ml_dtypes.bfloat16).astype(np.float64), axis, -1)
    blocks = v.reshape(v.shape[:-1] + (-1, 32))
    amax = np.abs(blocks).max(-1, keepdims=True)
    byte = np.maximum(np.where(amax > 0, np.frexp(amax)[1] - 1 + 127, 0) - down, 1)
    scale = np.exp2(byte - 127.0)
    codes = (blocks / scale).astype(np.float32).astype(dtype).astype(np.float64)
    return np.moveaxis((codes * scale).reshape(v.shape), -1, axis)


WIDE = False


def mx_kscale(k):
    if not WIDE:
        return np.ones(k)
    levels = np.array([10, -10, 5, -5, 0])
    if k % 512:
        return np.exp2(np.random.permutation(np.resize(levels, k // 32))).repeat(32)
    a = np.empty((k // 512, 16))
    for p in range(k // 512):
        a[p, :8] = np.random.permutation(np.resize(levels, 8))
        for g in range(8):
            far = levels[np.abs(levels - a[p, g]) >= 10]
            a[p, g + 8] = far[np.random.randint(len(far))]
    return np.exp2(a.ravel()).repeat(32)


def f64(x):
    return np.asarray(x).astype(np.float64)


def striped(idx):
    return np.tile(np.asarray(idx).reshape(-1, 16).T, (8, 1)).astype(np.uint16)


def unstriped(offs):
    return offs[:16].T.reshape(-1).astype(np.int64)


E2M1 = np.array([0.0, 0.5, 1.0, 1.5, 2.0, 3.0, 4.0, 6.0, -0.0, -0.5, -1.0, -1.5, -2.0, -3.0, -4.0, -6.0])


def pack_weight(w, fmt):
    k, n = w.shape
    w = f64(np.asarray(w, np.float32).astype(ml_dtypes.bfloat16)).reshape(k // 32, 32, n)
    amax = np.abs(w).max(1)
    if fmt == "e4m3":
        byte = np.frexp(amax)[1] - 1 + 127 - 7
    else:
        mant, ex = np.frexp(amax / 6.0)
        byte = np.where(mant > 0.5, ex, ex - 1) + 127
    byte = np.clip(np.where(amax > 0, byte, 1), 1, 254)
    scaled = (w * np.exp2(127.0 - byte)[:, None, :]).reshape(k, n).astype(np.float32)
    by_word = np.ascontiguousarray(scaled.reshape(k // 512, 128, 4, n).transpose(0, 1, 3, 2))
    if fmt == "e4m3":
        words = by_word.astype(ml_dtypes.float8_e4m3fn).view(np.uint8)
    else:
        c = by_word.astype(ml_dtypes.float4_e2m1fn).view(np.uint8) & 0xF
        words = (c[..., 0::2] | (c[..., 1::2] << 4)).reshape(k // 512, 128, 2 * n)
    return np.ascontiguousarray(words), np.ascontiguousarray(byte.astype(np.uint8).reshape(k // 512, 16, n))


def unpack_weight(words, scales, fmt):
    g, _, n = scales.shape
    words = np.ascontiguousarray(words).reshape(g, 128, n, -1)
    if fmt == "e4m3":
        vals = words.view(ml_dtypes.float8_e4m3fn).astype(np.float64)
    else:
        nib = np.empty((g, 128, n, 4), np.uint8)
        nib[..., 0::2] = words & 0xF
        nib[..., 1::2] = words >> 4
        vals = E2M1[nib]
    vals = vals * np.repeat(np.exp2(scales.astype(np.float64) - 127.0), 8, axis=1)[..., None]
    return vals.transpose(0, 1, 3, 2).reshape(g * 512, n)


D, T, I, Q, E, N, G = 512, 2048, 512, 128, 512, 32, 64


def setup_inputs():
    n = np.random.standard_normal
    idx = np.random.permutation(T)[:I]
    fd = mx_kscale(D)
    fi = mx_kscale(I)
    ti = np.ones(T)
    ti[idx] = fi
    keysp = pack_weight(n((D, T)) / fd[:, None], "e4m3")
    return {
        "query": (n((D, Q)) * 0.7 / np.sqrt(D) * fd[:, None]).astype(np.float32),
        "query2": (n((D, Q)) * 0.9 / np.sqrt(D) * fd[:, None]).astype(np.float32),
        "keys_words": keysp[0],
        "keys_scales": keysp[1],
        "lam": (np.random.uniform(0.3, 0.9, (Q, 1))).astype(np.float32),
        "mix": (np.random.uniform(0.2, 0.8, (Q, 1))).astype(np.float32),
        "os": (np.random.uniform(4.0, 16.0, (1, I)) * fi).astype(np.float32),
        "vals": (n((E, T)) / ti).astype(np.float32),
        "before": (n((Q, E))).astype(np.float32),
        "hold": (np.random.uniform(0.1, 0.6, (Q, 1))).astype(np.float32),
        "offs": striped(idx),
    }


def reference(query, query2, keys_words, keys_scales, lam, mix, os, vals, before, hold, offs):
    idx = unstriped(offs)
    keysu = unpack_weight(keys_words, keys_scales, "e4m3")
    queryq = mxq(f64(query), 0, "e4m3")
    keysidxg = keysu[:, idx]
    a = queryq.T @ keysidxg
    query2q = mxq(f64(query2), 0, "e4m3")
    b = query2q.T @ keysidxg
    mb = b.reshape(Q, N, I // N).max(axis=2)
    mr = np.repeat(mb, I // N, axis=1)
    s = a + mr * f64(lam)
    p = np.exp(s - np.max(s, axis=1, keepdims=True))
    r = p / np.sum(p, axis=1, keepdims=True)
    pm = r.reshape(Q, G, I // G).mean(axis=2)
    pr = np.repeat(pm, I // G, axis=1)
    w = r * (1.0 - f64(mix)) + pr * f64(mix)
    wo1 = w * f64(os)
    wt1 = wo1.T
    vt1 = f64(vals)[:, idx].T
    wt1q = mxq(wt1, 0, "e4m3")
    vt1q = mxq(vt1, 0, "e4m3")
    o = wt1q.T @ vt1q
    y = f64(before) * f64(hold) + o * (1.0 - f64(hold))
    return y

@@ -1,0 +1,192 @@
+from contextlib import ExitStack
+
+import concourse.mybir as mybir
+from concourse.masks import make_identity
+
+D, T, I, Q, E = 512, 2048, 512, 128, 512
+PAGE, RUN = 16, 8
+P, PACK = 128, 4
+FLOPS = 2 * Q * I * (2 * D + E)
+
+F32 = mybir.dt.float32
+BF16 = mybir.dt.bfloat16
+I32 = mybir.dt.int32
+U32 = mybir.dt.uint32
+U16 = mybir.dt.uint16
+U8 = mybir.dt.uint8
+FP8X4 = mybir.dt.float8_e4m3fn_x4
+ALU = mybir.AluOpType
+ACT = mybir.ActivationFunctionType
+AXIS = mybir.AxisListType
+
+
+def tile_attend_pagelift_smoothpage_blend_kernel(
+    tc, query, query2, keys_words, keys_scales, lam, mix, slot_factor, vals, before, hold, offs, out
+):
+    nc = tc.nc
+    n_pages = I // PAGE
+    n_runs = I // RUN
+    n_blocks = E // P
+
+    with ExitStack() as ctx:
+        lists = ctx.enter_context(tc.tile_pool(name="lists", bufs=1))
+        sb = ctx.enter_context(tc.tile_pool(name="sb", bufs=1))
+        ps = ctx.enter_context(tc.psum_pool(name="ps", bufs=1))
+
+        offsets = lists.tile([P, I // 16], U16, name="offsets")
+        nc.sync.dma_start(offsets[:], offs)
+
+        key_bytes = sb.tile([P, T], U8, name="key_bytes", align_bytes=64)
+        nc.gpsimd.memset(key_bytes[:].bitcast(I32), 0)
+        for r in range(4):
+            nc.scalar.dma_start(key_bytes[r:P:32, :].bitcast(I32), keys_scales[0, r:16:4, :].bitcast(I32))
+
+        key_words = sb.tile([P, T], U32, name="key_words", align_bytes=64)
+        nc.sync.dma_start(key_words[:].bitcast(I32), keys_words[0].rearrange("p t r -> p (t r)").bitcast(I32))
+
+        q_raw = []
+        for name, src in (("query2", query2), ("query", query)):
+            raw = sb.tile([P, PACK, Q], F32, name=name + "_raw")
+            nc.sync.dma_start(raw[:], src.rearrange("(p j) q -> p j q", j=PACK))
+            q_raw.append(raw)
+
+        lam_sb = sb.tile([P, 1], F32, name="lam_sb")
+        nc.gpsimd.dma_start(lam_sb[:], lam)
+        mix_sb = sb.tile([P, 1], F32, name="mix_sb")
+        nc.gpsimd.dma_start(mix_sb[:], mix)
+        os_sb = sb.tile([P, PACK], F32, name="os_sb")
+        nc.gpsimd.dma_start(os_sb[:], slot_factor.rearrange("o (p t) -> p (o t)", t=PACK))
+        hold_sb = sb.tile([P, 1], F32, name="hold_sb")
+        nc.gpsimd.dma_start(hold_sb[:], hold)
+
+        val_rows = []
+        for j in range(n_blocks):
+            rows = sb.tile([P, T], F32, name="val_rows%d" % j, tag="val_rows%d" % j, align_bytes=64)
+            nc.sync.dma_start(rows[:], vals[j * P : (j + 1) * P, :])
+            val_rows.append(rows)
+        before_sb = sb.tile([P, E], F32, name="before_sb")
+        nc.sync.dma_start(before_sb[:], before)
+
+        identity = sb.tile([P, P], F32, name="identity")
+        make_identity(nc, identity[:])
+
+        zero = sb.tile([P, 1], F32, name="zero")
+        nc.gpsimd.memset(zero[:], 0.0)
+        one = sb.tile([P, 1], F32, name="one")
+        nc.scalar.activation(one[:], zero[:], ACT.Exp)
+        own_share = sb.tile([P, 1], F32, name="own_share")
+        nc.gpsimd.tensor_scalar(own_share[:], mix_sb[:], -1.0, one[:], ALU.mult, ALU.add)
+        run_share = sb.tile([P, 1], F32, name="run_share")
+        nc.gpsimd.tensor_scalar(run_share[:], mix_sb[:], 1.0 / RUN, 0.0, ALU.mult, ALU.add)
+        new_share = sb.tile([P, 1], F32, name="new_share")
+        nc.gpsimd.tensor_scalar(new_share[:], hold_sb[:], -1.0, one[:], ALU.mult, ALU.add)
+
+        k_scales = sb.tile([P, I], U8, name="k_scales", align_bytes=64)
+        nc.vector.tensor_copy(k_scales[:], key_bytes[:].indirect(offsets[:]))
+        k_codes = sb.tile([P, I], U32, name="k_codes", align_bytes=64)
+        nc.vector.tensor_copy(k_codes[:], key_words[:].indirect(offsets[:]))
+
+        scores = []
+        for n, raw in enumerate(q_raw):
+            grouped = sb.tile([P, Q, PACK], BF16, name="q_grouped%d" % n, align_bytes=64)
+            nc.scalar.copy(
+                grouped[:].rearrange("p (c i) j -> p c j i", i=4), raw[:].rearrange("p j (c i) -> p c j i", i=4)
+            )
+            codes = sb.tile([P, Q], U32, name="q_codes%d" % n, align_bytes=64)
+            scales = sb.tile([P, Q], U8, name="q_scales%d" % n, align_bytes=64)
+            nc.vector.quantize_mx(codes[:].bitcast(FP8X4), scales[:], grouped[:].rearrange("p q j -> p (q j)"))
+            bank = ps.tile([P, I], F32, name="score%d" % n)
+            nc.tensor.matmul_mx(
+                bank[:], lhsT=codes[:].bitcast(FP8X4), lhsT_scale=scales[:],
+                rhs=k_codes[:].bitcast(FP8X4), rhs_scale=k_scales[:], start=True, stop=True,
+            )
+            scores.append(bank)
+        b_bank, a_bank = scores
+
+        def gather_values(j):
+            picked = sb.tile([P, I], BF16, name="picked%d" % j, align_bytes=64)
+            nc.vector.tensor_copy(picked[:], val_rows[j][:].indirect(offsets[:]))
+            return picked
+
+        page_max = sb.tile([P, n_pages], F32, name="page_max")
+        nc.vector.tensor_reduce(page_max[:], b_bank[:].rearrange("q (n i) -> q n i", i=PAGE), AXIS.X, ALU.max)
+        s = sb.tile([P, I], F32, name="s")
+        nc.vector.scalar_tensor_tensor(
+            s[:].rearrange("q (n i) -> q n i", i=PAGE),
+            page_max[:].unsqueeze(2).to_broadcast([P, n_pages, PAGE]),
+            lam_sb[:],
+            a_bank[:].rearrange("q (n i) -> q n i", i=PAGE),
+            ALU.mult, ALU.add,
+        )
+        neg_max = sb.tile([P, 1], F32, name="neg_max")
+        nc.vector.tensor_reduce(neg_max[:], s[:], AXIS.X, ALU.max, negate=True)
+        p = sb.tile([P, I], F32, name="p")
+        row_sum = sb.tile([P, 1], F32, name="row_sum")
+        nc.scalar.activation(p[:], s[:], ACT.Exp, bias=neg_max[:], scale=1.0, accum_out=row_sum[:])
+        gathered = [gather_values(0)]
+        inv_sum = sb.tile([P, 1], F32, name="inv_sum", tag="val_rows0", align_bytes=64)
+        nc.vector.reciprocal(inv_sum[:], row_sum[:])
+        own_factor = sb.tile([P, 1], F32, name="own_factor", tag="v_grouped0", align_bytes=64)
+        nc.scalar.activation(own_factor[:], inv_sum[:], ACT.Copy, scale=own_share[:])
+        own_term = sb.tile([P, PACK, P], F32, name="own_term")
+        nc.scalar.activation(
+            own_term[:].rearrange("q t (c i) -> q c t i", i=4),
+            p[:].rearrange("q (c i t) -> q c t i", i=4, t=PACK),
+            ACT.Copy, scale=own_factor[:],
+        )
+        run_sum = sb.tile([P, n_runs], F32, name="run_sum")
+        nc.vector.tensor_reduce(run_sum[:], p[:].rearrange("q (g j) -> q g j", j=RUN), AXIS.X, ALU.add)
+        run_term = sb.tile([P, P], F32, name="run_term")
+        nc.vector.tensor_scalar(
+            run_term[:].rearrange("q (g h) -> q g h", g=n_runs),
+            run_sum[:].unsqueeze(2).to_broadcast([P, n_runs, P // n_runs]),
+            inv_sum[:], run_share[:], ALU.mult, ALU.mult,
+        )
+        w_bank = ps.tile([P, PACK, Q], F32, name="w_bank")
+        for t in range(PACK):
+            nc.tensor.matmul(w_bank[:, t, :], own_term[:, t, :], identity[:], start=True, stop=False, is_transpose=True)
+            nc.tensor.matmul(w_bank[:, t, :], run_term[:], identity[:], start=False, stop=True, is_transpose=True)
+        gathered.append(gather_values(1))
+        w_grouped = sb.tile([P, Q, PACK], BF16, name="w_grouped", tag="val_rows1", align_bytes=64)
+        nc.vector.tensor_tensor(
+            w_grouped[:], w_bank[:].rearrange("m t q -> m q t"),
+            os_sb[:].unsqueeze(1).to_broadcast([P, Q, PACK]), ALU.mult,
+        )
+        gathered.append(gather_values(2))
+        w_codes = sb.tile([P, Q], U32, name="w_codes", tag="val_rows2", align_bytes=64)
+        w_scales = sb.tile([P, Q], U8, name="w_scales", align_bytes=64)
+        nc.vector.quantize_mx(w_codes[:].bitcast(FP8X4), w_scales[:], w_grouped[:].rearrange("m q t -> m (q t)"))
+
+        gathered.append(gather_values(3))
+        kept = sb.tile([P, E], F32, name="kept")
+        nc.scalar.activation(kept[:], before_sb[:], ACT.Copy, scale=hold_sb[:])
+        head = (n_blocks - 1) * P
+        o_head = ps.tile([P, head], F32, name="o_head")
+        o_tail = ps.tile([P, P], F32, name="o_tail")
+        v_grouped = []
+        for j in range(n_blocks):
+            picked = gathered[j]
+            pairs = picked[:].bitcast(F32)
+            v_bank = ps.tile([P, 2, P], F32, name="v_bank", tag="v_bank", bufs=2)
+            for u in range(2):
+                nc.tensor.transpose(v_bank[:, u, :], pairs[:, u : I // 2 : 2], identity[:])
+            grouped = sb.tile([P, P * PACK], BF16, name="v_grouped%d" % j, tag="v_grouped%d" % j, align_bytes=64)
+            nc.scalar.copy(
+                grouped[:].bitcast(F32).rearrange("m (e u) -> m e u", u=2),
+                v_bank[:].rearrange("m u e -> m e u"),
+            )
+            v_grouped.append(grouped)
+        for j in range(n_blocks):
+            v_codes = sb.tile([P, P], U32, name="v_codes%d" % j, align_bytes=64)
+            v_scales = sb.tile([P, P], U8, name="v_scales%d" % j, align_bytes=64)
+            nc.vector.quantize_mx(v_codes[:].bitcast(FP8X4), v_scales[:], v_grouped[j][:])
+            target = o_head[:, j * P : (j + 1) * P] if j < n_blocks - 1 else o_tail[:]
+            nc.tensor.matmul_mx(
+                target, lhsT=w_codes[:].bitcast(FP8X4), lhsT_scale=w_scales[:],
+                rhs=v_codes[:].bitcast(FP8X4), rhs_scale=v_scales[:], start=True, stop=True,
+            )
+
+        for bank, cols in ((o_head, slice(0, head)), (o_tail, slice(head, E))):
+            result = sb.tile([P, cols.stop - cols.start], F32, name="result%d" % cols.start)
+            nc.vector.scalar_tensor_tensor(result[:], bank[:], new_share[:], kept[:, cols], ALU.mult, ALU.add)
+            nc.sync.dma_start(out[:, cols], result[:])

@@ -31,111 +31,143 @@ def tile_attend_pagelift_smoothpage_blend_kernel(
     with ExitStack() as ctx:
         lists = ctx.enter_context(tc.tile_pool(name="lists", bufs=1))
         sb = ctx.enter_context(tc.tile_pool(name="sb", bufs=1))
+        placed = ctx.enter_context(tc.tile_pool(name="placed", bufs=1))
         ps = ctx.enter_context(tc.psum_pool(name="ps", bufs=1))
 
-        offsets = lists.tile([P, I // 16], U16, name="offsets")
-        nc.sync.dma_start(offsets[:], offs)
-
-        key_bytes = sb.tile([P, T], U8, name="key_bytes", align_bytes=64)
-        nc.gpsimd.memset(key_bytes[:].bitcast(I32), 0)
-        for r in range(4):
-            nc.scalar.dma_start(key_bytes[r:P:32, :].bitcast(I32), keys_scales[0, r:16:4, :].bitcast(I32))
-
-        key_words = sb.tile([P, T], U32, name="key_words", align_bytes=64)
-        nc.sync.dma_start(key_words[:].bitcast(I32), keys_words[0].rearrange("p t r -> p (t r)").bitcast(I32))
-
         q_raw = []
-        for name, src in (("query2", query2), ("query", query)):
-            raw = sb.tile([P, PACK, Q], F32, name=name + "_raw")
+        for name, src, tag in (("query2_raw", query2, "vectors"), ("query_raw", query, "first_rows1")):
+            raw = sb.tile([P, PACK, Q], F32, name=name, tag=tag, align_bytes=64)
             nc.sync.dma_start(raw[:], src.rearrange("(p j) q -> p j q", j=PACK))
             q_raw.append(raw)
 
-        lam_sb = sb.tile([P, 1], F32, name="lam_sb")
-        nc.gpsimd.dma_start(lam_sb[:], lam)
-        mix_sb = sb.tile([P, 1], F32, name="mix_sb")
-        nc.gpsimd.dma_start(mix_sb[:], mix)
-        os_sb = sb.tile([P, PACK], F32, name="os_sb")
-        nc.gpsimd.dma_start(os_sb[:], slot_factor.rearrange("o (p t) -> p (o t)", t=PACK))
-        hold_sb = sb.tile([P, 1], F32, name="hold_sb")
-        nc.gpsimd.dma_start(hold_sb[:], hold)
+        key_bytes = sb.tile([P, T], U8, name="key_bytes", tag="key_bytes", align_bytes=64)
+        nc.vector.memset(key_bytes[:].bitcast(I32), 0)
+        for r in range(4):
+            queue = nc.sync if r >= 2 else nc.scalar
+            queue.dma_start(key_bytes[r:P:32, :].bitcast(I32), keys_scales[0, r:16:4, :].bitcast(I32))
+        offsets = lists.tile([P, I // 16], U16, name="offsets")
+        nc.sync.dma_start(offsets[:], offs)
 
-        val_rows = []
-        for j in range(n_blocks):
-            rows = sb.tile([P, T], F32, name="val_rows%d" % j, tag="val_rows%d" % j, align_bytes=64)
-            nc.sync.dma_start(rows[:], vals[j * P : (j + 1) * P, :])
-            val_rows.append(rows)
-        before_sb = sb.tile([P, E], F32, name="before_sb")
-        nc.sync.dma_start(before_sb[:], before)
-
+        run_length = sb.tile([P, 1], F32, name="run_length", tag="val_rows2", align_bytes=64)
+        nc.vector.memset(run_length[:], float(RUN))
+        inv_run = sb.tile([P, 1], F32, name="inv_run")
+        nc.vector.reciprocal(inv_run[:], run_length[:])
+        zero = sb.tile([P, 1], F32, name="zero", tag="val_rows3", align_bytes=64)
+        nc.vector.memset(zero[:], 0.0)
+        one = sb.tile([P, 1], F32, name="one")
+        nc.scalar.activation(one[:], zero[:], ACT.Exp)
         identity = sb.tile([P, P], F32, name="identity")
         make_identity(nc, identity[:])
 
-        zero = sb.tile([P, 1], F32, name="zero")
-        nc.gpsimd.memset(zero[:], 0.0)
-        one = sb.tile([P, 1], F32, name="one")
-        nc.scalar.activation(one[:], zero[:], ACT.Exp)
-        own_share = sb.tile([P, 1], F32, name="own_share")
-        nc.gpsimd.tensor_scalar(own_share[:], mix_sb[:], -1.0, one[:], ALU.mult, ALU.add)
-        run_share = sb.tile([P, 1], F32, name="run_share")
-        nc.gpsimd.tensor_scalar(run_share[:], mix_sb[:], 1.0 / RUN, 0.0, ALU.mult, ALU.add)
-        new_share = sb.tile([P, 1], F32, name="new_share")
-        nc.gpsimd.tensor_scalar(new_share[:], hold_sb[:], -1.0, one[:], ALU.mult, ALU.add)
+        key_words = sb.tile([P, T], U32, name="key_words", tag="val_rows2", align_bytes=64)
+        nc.sync.dma_start(key_words[:].bitcast(I32), keys_words[0].rearrange("p t r -> p (t r)").bitcast(I32))
 
         k_scales = sb.tile([P, I], U8, name="k_scales", align_bytes=64)
         nc.vector.tensor_copy(k_scales[:], key_bytes[:].indirect(offsets[:]))
-        k_codes = sb.tile([P, I], U32, name="k_codes", align_bytes=64)
-        nc.vector.tensor_copy(k_codes[:], key_words[:].indirect(offsets[:]))
 
-        scores = []
+        q_grouped = placed.tile([P, 2, Q, PACK], BF16, name="q_grouped", offset=0, align_bytes=64)
         for n, raw in enumerate(q_raw):
-            grouped = sb.tile([P, Q, PACK], BF16, name="q_grouped%d" % n, align_bytes=64)
             nc.scalar.copy(
-                grouped[:].rearrange("p (c i) j -> p c j i", i=4), raw[:].rearrange("p j (c i) -> p c j i", i=4)
+                q_grouped[:, n].rearrange("p (c i) j -> p c j i", i=4), raw[:].rearrange("p j (c i) -> p c j i", i=4)
             )
-            codes = sb.tile([P, Q], U32, name="q_codes%d" % n, align_bytes=64)
-            scales = sb.tile([P, Q], U8, name="q_scales%d" % n, align_bytes=64)
-            nc.vector.quantize_mx(codes[:].bitcast(FP8X4), scales[:], grouped[:].rearrange("p q j -> p (q j)"))
-            bank = ps.tile([P, I], F32, name="score%d" % n)
-            nc.tensor.matmul_mx(
-                bank[:], lhsT=codes[:].bitcast(FP8X4), lhsT_scale=scales[:],
-                rhs=k_codes[:].bitcast(FP8X4), rhs_scale=k_scales[:], start=True, stop=True,
-            )
-            scores.append(bank)
-        b_bank, a_bank = scores
+        q_codes = sb.tile([P, 2 * Q], U32, name="q_codes", tag="key_bytes", align_bytes=64)
+        q_scales = sb.tile([P, 2 * Q], U8, name="q_scales", align_bytes=64)
+        nc.vector.quantize_mx(q_codes[:].bitcast(FP8X4), q_scales[:], q_grouped[:].rearrange("p n q j -> p (n q j)"))
 
-        def gather_values(j):
-            picked = sb.tile([P, I], BF16, name="picked%d" % j, align_bytes=64)
+        half = I // 2
+        page_max = sb.tile([P, 2, 2, n_pages // 2], F32, name="page_max")
+        banks = []
+        for h in range(2):
+            slots = slice(h * half, (h + 1) * half)
+            k_codes = placed.tile([P, half], U32, name="k_codes%d" % h, offset=(0, 9216)[h], align_bytes=64)
+            nc.vector.tensor_copy(k_codes[:], key_words[:].indirect(offsets[:, h * half // 16 : (h + 1) * half // 16]))
+            bank = ps.tile([P, 2, half], F32, name="score%d" % h)
+            for n in range(2):
+                rows = slice(n * Q, (n + 1) * Q)
+                nc.tensor.matmul_mx(
+                    bank[:, n, :], lhsT=q_codes[:, rows].bitcast(FP8X4), lhsT_scale=q_scales[:, rows],
+                    rhs=k_codes[:].bitcast(FP8X4), rhs_scale=k_scales[:, slots], start=True, stop=True,
+                )
+            banks.append(bank)
+
+        def load_values(name, tag, src):
+            rows = sb.tile([P, src.shape[1]], F32, name=name, tag=tag, align_bytes=64)
+            nc.sync.dma_start(rows[:], src)
+            return rows
+
+        first_rows = [load_values("first_rows0", "val_rows3", vals[0:P, : T // 2])]
+        vectors = sb.tile([P, 3, 8], F32, name="vectors", tag="vectors", align_bytes=64)
+        lam_sb, mix_sb, hold_sb = vectors[:, 0, 0:1], vectors[:, 1, 0:1], vectors[:, 2, 0:1]
+        for column, src in ((lam_sb, lam), (mix_sb, mix), (hold_sb, hold)):
+            nc.sync.dma_start(column, src)
+        first_rows.append(load_values("first_rows1", "first_rows1", vals[0:P, T // 2 :]))
+        rows1 = placed.tile([P, T], F32, name="val_rows1", offset=1024, align_bytes=64)
+        nc.sync.dma_start(rows1[:], vals[P : 2 * P, :])
+        val_rows = {1: rows1, 2: load_values("val_rows2", "val_rows2", vals[2 * P : 3 * P, :])}
+        os_sb = placed.tile([P, PACK], F32, name="os_sb", offset=0, align_bytes=64)
+        nc.sync.dma_start(os_sb[:], slot_factor.rearrange("o (p t) -> p (o t)", t=PACK))
+
+        own_share = sb.tile([P, 1], F32, name="own_share")
+        nc.gpsimd.tensor_scalar(own_share[:], mix_sb, -1.0, one[:], ALU.mult, ALU.add)
+        run_share = sb.tile([P, 1], F32, name="run_share")
+        nc.gpsimd.tensor_scalar(run_share[:], mix_sb, inv_run[:], 0.0, ALU.mult, ALU.add)
+        new_share = sb.tile([P, 1], F32, name="new_share")
+        nc.gpsimd.tensor_scalar(new_share[:], hold_sb, -1.0, one[:], ALU.mult, ALU.add)
+
+        for h in range(2):
+            nc.vector.tensor_reduce(
+                page_max[:, h].rearrange("q s n -> q (s n)"),
+                banks[h][:].rearrange("q s (n i) -> q (s n) i", i=PAGE), AXIS.X, ALU.max,
+            )
+        b_max, a_max = page_max[:, :, 0, :], page_max[:, :, 1, :]
+
+        def gather_values(j, tag):
+            picked = sb.tile([P, I], BF16, name="picked%d" % j, tag=tag, align_bytes=64)
             nc.vector.tensor_copy(picked[:], val_rows[j][:].indirect(offsets[:]))
             return picked
 
-        page_max = sb.tile([P, n_pages], F32, name="page_max")
-        nc.vector.tensor_reduce(page_max[:], b_bank[:].rearrange("q (n i) -> q n i", i=PAGE), AXIS.X, ALU.max)
-        s = sb.tile([P, I], F32, name="s")
-        nc.vector.scalar_tensor_tensor(
-            s[:].rearrange("q (n i) -> q n i", i=PAGE),
-            page_max[:].unsqueeze(2).to_broadcast([P, n_pages, PAGE]),
-            lam_sb[:],
-            a_bank[:].rearrange("q (n i) -> q n i", i=PAGE),
-            ALU.mult, ALU.add,
+        rounded = sb.tile([P, T], BF16, name="rounded", tag="picked2", align_bytes=64)
+        for h in range(2):
+            nc.scalar.activation(rounded[:, h * (T // 2) : (h + 1) * (T // 2)], first_rows[h][:], ACT.Copy)
+        val_rows[3] = load_values("val_rows3", "val_rows3", vals[3 * P :, :])
+        before_sb = sb.tile([P, E], F32, name="before_sb", tag="first_rows1", align_bytes=64)
+        nc.sync.dma_start(before_sb[:], before)
+
+
+        picked0 = sb.tile([P, I], BF16, name="picked0", align_bytes=64)
+        nc.scalar.activation(picked0[:], rounded[:].indirect(offsets[:]), ACT.Copy)
+
+        lift = sb.tile([P, P], F32, name="lift")
+        nc.vector.tensor_scalar(
+            lift[:].rearrange("q (h n c) -> q h n c", h=2, n=n_pages // 2),
+            b_max.unsqueeze(3).to_broadcast([P, 2, n_pages // 2, P // n_pages]),
+            lam_sb, None, ALU.mult,
         )
+        s_max = sb.tile([P, 2, n_pages // 2], F32, name="s_max", tag="picked1", align_bytes=64)
+        nc.vector.scalar_tensor_tensor(s_max[:], b_max, lam_sb, a_max, ALU.mult, ALU.add)
+        s = sb.tile([P, PACK, P], F32, name="s")
+        for h in range(2):
+            cols = slice(h * P // 2, (h + 1) * P // 2)
+            nc.vector.tensor_tensor(
+                s[:, :, cols], banks[h][:, 1, :].rearrange("q (m t) -> q t m", t=PACK),
+                lift[:, cols].unsqueeze(1).to_broadcast([P, PACK, P // 2]), ALU.add,
+            )
         neg_max = sb.tile([P, 1], F32, name="neg_max")
-        nc.vector.tensor_reduce(neg_max[:], s[:], AXIS.X, ALU.max, negate=True)
-        p = sb.tile([P, I], F32, name="p")
+        nc.vector.tensor_reduce(neg_max[:], s_max[:].rearrange("q h n -> q (h n)"), AXIS.X, ALU.max, negate=True)
+        p = sb.tile([P, I], F32, name="p", tag="picked2", align_bytes=64)
         row_sum = sb.tile([P, 1], F32, name="row_sum")
-        nc.scalar.activation(p[:], s[:], ACT.Exp, bias=neg_max[:], scale=1.0, accum_out=row_sum[:])
-        gathered = [gather_values(0)]
-        inv_sum = sb.tile([P, 1], F32, name="inv_sum", tag="val_rows0", align_bytes=64)
-        nc.vector.reciprocal(inv_sum[:], row_sum[:])
-        own_factor = sb.tile([P, 1], F32, name="own_factor", tag="v_grouped0", align_bytes=64)
-        nc.scalar.activation(own_factor[:], inv_sum[:], ACT.Copy, scale=own_share[:])
-        own_term = sb.tile([P, PACK, P], F32, name="own_term")
         nc.scalar.activation(
-            own_term[:].rearrange("q t (c i) -> q c t i", i=4),
-            p[:].rearrange("q (c i t) -> q c t i", i=4, t=PACK),
-            ACT.Copy, scale=own_factor[:],
+            p[:], s[:].rearrange("q t m -> q (t m)"), ACT.Exp, bias=neg_max[:], scale=1.0, accum_out=row_sum[:]
         )
+        picked1 = gather_values(1, "picked1")
+        inv_sum = placed.tile([P, 1], F32, name="inv_sum", offset=1024, align_bytes=64)
+        nc.vector.reciprocal(inv_sum[:], row_sum[:])
         run_sum = sb.tile([P, n_runs], F32, name="run_sum")
-        nc.vector.tensor_reduce(run_sum[:], p[:].rearrange("q (g j) -> q g j", j=RUN), AXIS.X, ALU.add)
+        nc.vector.tensor_reduce(
+            run_sum[:], p[:].rearrange("q (t g h) -> q g t h", t=PACK, g=n_runs), AXIS.XY, ALU.add
+        )
+        own_term = sb.tile([P, I], F32, name="own_term")
+        nc.vector.tensor_scalar(own_term[:], p[:], inv_sum[:], own_share[:], ALU.mult, ALU.mult)
         run_term = sb.tile([P, P], F32, name="run_term")
         nc.vector.tensor_scalar(
             run_term[:].rearrange("q (g h) -> q g h", g=n_runs),
@@ -144,48 +176,63 @@ def tile_attend_pagelift_smoothpage_blend_kernel(
         )
         w_bank = ps.tile([P, PACK, Q], F32, name="w_bank")
         for t in range(PACK):
-            nc.tensor.matmul(w_bank[:, t, :], own_term[:, t, :], identity[:], start=True, stop=False, is_transpose=True)
-            nc.tensor.matmul(w_bank[:, t, :], run_term[:], identity[:], start=False, stop=True, is_transpose=True)
-        gathered.append(gather_values(1))
-        w_grouped = sb.tile([P, Q, PACK], BF16, name="w_grouped", tag="val_rows1", align_bytes=64)
+            nc.tensor.matmul(
+                w_bank[:, t, :], own_term[:, t * P : (t + 1) * P], identity[:],
+                start=(t == 0), stop=False, is_transpose=True,
+            )
+        for t in range(PACK):
+            nc.tensor.matmul(
+                w_bank[:, t, :], run_term[:], identity[:], start=False, stop=(t == PACK - 1), is_transpose=True
+            )
+        picked2 = gather_values(2, "picked2")
+
+        def turn_values(picked, grouped):
+            pairs = picked[:].bitcast(F32)
+            v_bank = ps.tile([P, 2, P], F32, name="v_bank", tag="v_bank", bufs=3)
+            for u in range(2):
+                nc.tensor.transpose(v_bank[:, u, :], pairs[:, u : I // 2 : 2], identity[:])
+            nc.scalar.copy(
+                grouped.bitcast(F32).rearrange("m (e u) -> m e u", u=2), v_bank[:].rearrange("m u e -> m e u")
+            )
+
+        def quantise(name, grouped, tag):
+            width = grouped.shape[1] // PACK
+            codes = sb.tile([P, width], U32, name=name + "_codes", tag=tag, align_bytes=64)
+            scales = sb.tile([P, width], U8, name=name + "_scales", align_bytes=64)
+            nc.vector.quantize_mx(codes[:].bitcast(FP8X4), scales[:], grouped)
+            return codes, scales
+
+        v01_grouped = sb.tile([P, 2 * P * PACK], BF16, name="v01_grouped", tag="grouped", align_bytes=64)
+        turn_values(picked0, v01_grouped[:, : P * PACK])
+        turn_values(picked1, v01_grouped[:, P * PACK :])
+        v01 = quantise("v01", v01_grouped[:], "val_rows2")
+
+        w_grouped = sb.tile([P, Q, PACK], BF16, name="w_grouped", tag="grouped", align_bytes=64)
         nc.vector.tensor_tensor(
             w_grouped[:], w_bank[:].rearrange("m t q -> m q t"),
             os_sb[:].unsqueeze(1).to_broadcast([P, Q, PACK]), ALU.mult,
         )
-        gathered.append(gather_values(2))
-        w_codes = sb.tile([P, Q], U32, name="w_codes", tag="val_rows2", align_bytes=64)
-        w_scales = sb.tile([P, Q], U8, name="w_scales", align_bytes=64)
-        nc.vector.quantize_mx(w_codes[:].bitcast(FP8X4), w_scales[:], w_grouped[:].rearrange("m q t -> m (q t)"))
+        picked3 = placed.tile([P, I], BF16, name="picked3", offset=0, align_bytes=64)
+        nc.vector.tensor_copy(picked3[:], val_rows[3][:].indirect(offsets[:]))
+        w_codes, w_scales = quantise("w", w_grouped[:].rearrange("m q t -> m (q t)"), "val_rows3")
 
-        gathered.append(gather_values(3))
+        v2_grouped = sb.tile([P, P * PACK], BF16, name="v2_grouped", align_bytes=64)
+        turn_values(picked2, v2_grouped[:])
+        v2 = quantise("v2", v2_grouped[:], "grouped")
         kept = sb.tile([P, E], F32, name="kept")
-        nc.scalar.activation(kept[:], before_sb[:], ACT.Copy, scale=hold_sb[:])
+        nc.scalar.activation(kept[:], before_sb[:], ACT.Copy, scale=hold_sb)
+        v3_grouped = sb.tile([P, P * PACK], BF16, name="v3_grouped", align_bytes=64)
+        turn_values(picked3, v3_grouped[:])
+        v3 = quantise("v3", v3_grouped[:], "v3_codes")
+
         head = (n_blocks - 1) * P
         o_head = ps.tile([P, head], F32, name="o_head")
         o_tail = ps.tile([P, P], F32, name="o_tail")
-        v_grouped = []
-        for j in range(n_blocks):
-            picked = gathered[j]
-            pairs = picked[:].bitcast(F32)
-            v_bank = ps.tile([P, 2, P], F32, name="v_bank", tag="v_bank", bufs=2)
-            for u in range(2):
-                nc.tensor.transpose(v_bank[:, u, :], pairs[:, u : I // 2 : 2], identity[:])
-            grouped = sb.tile([P, P * PACK], BF16, name="v_grouped%d" % j, tag="v_grouped%d" % j, align_bytes=64)
-            nc.scalar.copy(
-                grouped[:].bitcast(F32).rearrange("m (e u) -> m e u", u=2),
-                v_bank[:].rearrange("m u e -> m e u"),
-            )
-            v_grouped.append(grouped)
-        for j in range(n_blocks):
-            v_codes = sb.tile([P, P], U32, name="v_codes%d" % j, align_bytes=64)
-            v_scales = sb.tile([P, P], U8, name="v_scales%d" % j, align_bytes=64)
-            nc.vector.quantize_mx(v_codes[:].bitcast(FP8X4), v_scales[:], v_grouped[j][:])
-            target = o_head[:, j * P : (j + 1) * P] if j < n_blocks - 1 else o_tail[:]
+        for target, (codes, scales) in ((o_head[:, : 2 * P], v01), (o_head[:, 2 * P :], v2), (o_tail[:], v3)):
             nc.tensor.matmul_mx(
                 target, lhsT=w_codes[:].bitcast(FP8X4), lhsT_scale=w_scales[:],
-                rhs=v_codes[:].bitcast(FP8X4), rhs_scale=v_scales[:], start=True, stop=True,
+                rhs=codes[:].bitcast(FP8X4), rhs_scale=scales[:], start=True, stop=True,
             )
-
         for bank, cols in ((o_head, slice(0, head)), (o_tail, slice(head, E))):
             result = sb.tile([P, cols.stop - cols.start], F32, name="result%d" % cols.start)
             nc.vector.scalar_tensor_tensor(result[:], bank[:], new_share[:], kept[:, cols], ALU.mult, ALU.add)

from contextlib import ExitStack

import concourse.mybir as mybir
from concourse.masks import make_identity

D, T, I, Q, E = 512, 2048, 512, 128, 512
PAGE, RUN = 16, 8
P, PACK = 128, 4
FLOPS = 2 * Q * I * (2 * D + E)

F32 = mybir.dt.float32
BF16 = mybir.dt.bfloat16
I32 = mybir.dt.int32
U32 = mybir.dt.uint32
U16 = mybir.dt.uint16
U8 = mybir.dt.uint8
FP8X4 = mybir.dt.float8_e4m3fn_x4
ALU = mybir.AluOpType
ACT = mybir.ActivationFunctionType
AXIS = mybir.AxisListType


def tile_attend_pagelift_smoothpage_blend_kernel(
    tc, query, query2, keys_words, keys_scales, lam, mix, slot_factor, vals, before, hold, offs, out
):
    nc = tc.nc
    n_pages = I // PAGE
    n_runs = I // RUN
    n_blocks = E // P

    with ExitStack() as ctx:
        lists = ctx.enter_context(tc.tile_pool(name="lists", bufs=1))
        sb = ctx.enter_context(tc.tile_pool(name="sb", bufs=1))
        placed = ctx.enter_context(tc.tile_pool(name="placed", bufs=1))
        ps = ctx.enter_context(tc.psum_pool(name="ps", bufs=1))

        q_raw = []
        for name, src, tag in (("query2_raw", query2, "vectors"), ("query_raw", query, "first_rows1")):
            raw = sb.tile([P, PACK, Q], F32, name=name, tag=tag, align_bytes=64)
            nc.sync.dma_start(raw[:], src.rearrange("(p j) q -> p j q", j=PACK))
            q_raw.append(raw)

        key_bytes = sb.tile([P, T], U8, name="key_bytes", tag="key_bytes", align_bytes=64)
        nc.vector.memset(key_bytes[:].bitcast(I32), 0)
        for r in range(4):
            queue = nc.sync if r >= 2 else nc.scalar
            queue.dma_start(key_bytes[r:P:32, :].bitcast(I32), keys_scales[0, r:16:4, :].bitcast(I32))
        offsets = lists.tile([P, I // 16], U16, name="offsets")
        nc.sync.dma_start(offsets[:], offs)

        run_length = sb.tile([P, 1], F32, name="run_length", tag="val_rows2", align_bytes=64)
        nc.vector.memset(run_length[:], float(RUN))
        inv_run = sb.tile([P, 1], F32, name="inv_run")
        nc.vector.reciprocal(inv_run[:], run_length[:])
        zero = sb.tile([P, 1], F32, name="zero", tag="val_rows3", align_bytes=64)
        nc.vector.memset(zero[:], 0.0)
        one = sb.tile([P, 1], F32, name="one")
        nc.scalar.activation(one[:], zero[:], ACT.Exp)
        identity = sb.tile([P, P], F32, name="identity")
        make_identity(nc, identity[:])

        key_words = sb.tile([P, T], U32, name="key_words", tag="val_rows2", align_bytes=64)
        nc.sync.dma_start(key_words[:].bitcast(I32), keys_words[0].rearrange("p t r -> p (t r)").bitcast(I32))

        k_scales = sb.tile([P, I], U8, name="k_scales", align_bytes=64)
        nc.vector.tensor_copy(k_scales[:], key_bytes[:].indirect(offsets[:]))

        q_grouped = placed.tile([P, 2, Q, PACK], BF16, name="q_grouped", offset=0, align_bytes=64)
        for n, raw in enumerate(q_raw):
            nc.scalar.copy(
                q_grouped[:, n].rearrange("p (c i) j -> p c j i", i=4), raw[:].rearrange("p j (c i) -> p c j i", i=4)
            )
        q_codes = sb.tile([P, 2 * Q], U32, name="q_codes", tag="key_bytes", align_bytes=64)
        q_scales = sb.tile([P, 2 * Q], U8, name="q_scales", align_bytes=64)
        nc.vector.quantize_mx(q_codes[:].bitcast(FP8X4), q_scales[:], q_grouped[:].rearrange("p n q j -> p (n q j)"))

        half = I // 2
        page_max = sb.tile([P, 2, 2, n_pages // 2], F32, name="page_max")
        banks = []
        for h in range(2):
            slots = slice(h * half, (h + 1) * half)
            k_codes = placed.tile([P, half], U32, name="k_codes%d" % h, offset=(0, 9216)[h], align_bytes=64)
            nc.vector.tensor_copy(k_codes[:], key_words[:].indirect(offsets[:, h * half // 16 : (h + 1) * half // 16]))
            bank = ps.tile([P, 2, half], F32, name="score%d" % h)
            for n in range(2):
                rows = slice(n * Q, (n + 1) * Q)
                nc.tensor.matmul_mx(
                    bank[:, n, :], lhsT=q_codes[:, rows].bitcast(FP8X4), lhsT_scale=q_scales[:, rows],
                    rhs=k_codes[:].bitcast(FP8X4), rhs_scale=k_scales[:, slots], start=True, stop=True,
                )
            banks.append(bank)

        def load_values(name, tag, src):
            rows = sb.tile([P, src.shape[1]], F32, name=name, tag=tag, align_bytes=64)
            nc.sync.dma_start(rows[:], src)
            return rows

        first_rows = [load_values("first_rows0", "val_rows3", vals[0:P, : T // 2])]
        vectors = sb.tile([P, 3, 8], F32, name="vectors", tag="vectors", align_bytes=64)
        lam_sb, mix_sb, hold_sb = vectors[:, 0, 0:1], vectors[:, 1, 0:1], vectors[:, 2, 0:1]
        for column, src in ((lam_sb, lam), (mix_sb, mix), (hold_sb, hold)):
            nc.sync.dma_start(column, src)
        first_rows.append(load_values("first_rows1", "first_rows1", vals[0:P, T // 2 :]))
        rows1 = placed.tile([P, T], F32, name="val_rows1", offset=1024, align_bytes=64)
        nc.sync.dma_start(rows1[:], vals[P : 2 * P, :])
        val_rows = {1: rows1, 2: load_values("val_rows2", "val_rows2", vals[2 * P : 3 * P, :])}
        os_sb = placed.tile([P, PACK], F32, name="os_sb", offset=0, align_bytes=64)
        nc.sync.dma_start(os_sb[:], slot_factor.rearrange("o (p t) -> p (o t)", t=PACK))

        own_share = sb.tile([P, 1], F32, name="own_share")
        nc.gpsimd.tensor_scalar(own_share[:], mix_sb, -1.0, one[:], ALU.mult, ALU.add)
        run_share = sb.tile([P, 1], F32, name="run_share")
        nc.gpsimd.tensor_scalar(run_share[:], mix_sb, inv_run[:], 0.0, ALU.mult, ALU.add)
        new_share = sb.tile([P, 1], F32, name="new_share")
        nc.gpsimd.tensor_scalar(new_share[:], hold_sb, -1.0, one[:], ALU.mult, ALU.add)

        for h in range(2):
            nc.vector.tensor_reduce(
                page_max[:, h].rearrange("q s n -> q (s n)"),
                banks[h][:].rearrange("q s (n i) -> q (s n) i", i=PAGE), AXIS.X, ALU.max,
            )
        b_max, a_max = page_max[:, :, 0, :], page_max[:, :, 1, :]

        def gather_values(j, tag):
            picked = sb.tile([P, I], BF16, name="picked%d" % j, tag=tag, align_bytes=64)
            nc.vector.tensor_copy(picked[:], val_rows[j][:].indirect(offsets[:]))
            return picked

        rounded = sb.tile([P, T], BF16, name="rounded", tag="picked2", align_bytes=64)
        for h in range(2):
            nc.scalar.activation(rounded[:, h * (T // 2) : (h + 1) * (T // 2)], first_rows[h][:], ACT.Copy)
        val_rows[3] = load_values("val_rows3", "val_rows3", vals[3 * P :, :])
        before_sb = sb.tile([P, E], F32, name="before_sb", tag="first_rows1", align_bytes=64)
        nc.sync.dma_start(before_sb[:], before)


        picked0 = sb.tile([P, I], BF16, name="picked0", align_bytes=64)
        nc.scalar.activation(picked0[:], rounded[:].indirect(offsets[:]), ACT.Copy)

        lift = sb.tile([P, P], F32, name="lift")
        nc.vector.tensor_scalar(
            lift[:].rearrange("q (h n c) -> q h n c", h=2, n=n_pages // 2),
            b_max.unsqueeze(3).to_broadcast([P, 2, n_pages // 2, P // n_pages]),
            lam_sb, None, ALU.mult,
        )
        s_max = sb.tile([P, 2, n_pages // 2], F32, name="s_max", tag="picked1", align_bytes=64)
        nc.vector.scalar_tensor_tensor(s_max[:], b_max, lam_sb, a_max, ALU.mult, ALU.add)
        s = sb.tile([P, PACK, P], F32, name="s")
        for h in range(2):
            cols = slice(h * P // 2, (h + 1) * P // 2)
            nc.vector.tensor_tensor(
                s[:, :, cols], banks[h][:, 1, :].rearrange("q (m t) -> q t m", t=PACK),
                lift[:, cols].unsqueeze(1).to_broadcast([P, PACK, P // 2]), ALU.add,
            )
        neg_max = sb.tile([P, 1], F32, name="neg_max")
        nc.vector.tensor_reduce(neg_max[:], s_max[:].rearrange("q h n -> q (h n)"), AXIS.X, ALU.max, negate=True)
        p = sb.tile([P, I], F32, name="p", tag="picked2", align_bytes=64)
        row_sum = sb.tile([P, 1], F32, name="row_sum")
        nc.scalar.activation(
            p[:], s[:].rearrange("q t m -> q (t m)"), ACT.Exp, bias=neg_max[:], scale=1.0, accum_out=row_sum[:]
        )
        picked1 = gather_values(1, "picked1")
        inv_sum = placed.tile([P, 1], F32, name="inv_sum", offset=1024, align_bytes=64)
        nc.vector.reciprocal(inv_sum[:], row_sum[:])
        run_sum = sb.tile([P, n_runs], F32, name="run_sum")
        nc.vector.tensor_reduce(
            run_sum[:], p[:].rearrange("q (t g h) -> q g t h", t=PACK, g=n_runs), AXIS.XY, ALU.add
        )
        own_term = sb.tile([P, I], F32, name="own_term")
        nc.vector.tensor_scalar(own_term[:], p[:], inv_sum[:], own_share[:], ALU.mult, ALU.mult)
        run_term = sb.tile([P, P], F32, name="run_term")
        nc.vector.tensor_scalar(
            run_term[:].rearrange("q (g h) -> q g h", g=n_runs),
            run_sum[:].unsqueeze(2).to_broadcast([P, n_runs, P // n_runs]),
            inv_sum[:], run_share[:], ALU.mult, ALU.mult,
        )
        w_bank = ps.tile([P, PACK, Q], F32, name="w_bank")
        for t in range(PACK):
            nc.tensor.matmul(
                w_bank[:, t, :], own_term[:, t * P : (t + 1) * P], identity[:],
                start=(t == 0), stop=False, is_transpose=True,
            )
        for t in range(PACK):
            nc.tensor.matmul(
                w_bank[:, t, :], run_term[:], identity[:], start=False, stop=(t == PACK - 1), is_transpose=True
            )
        picked2 = gather_values(2, "picked2")

        def turn_values(picked, grouped):
            pairs = picked[:].bitcast(F32)
            v_bank = ps.tile([P, 2, P], F32, name="v_bank", tag="v_bank", bufs=3)
            for u in range(2):
                nc.tensor.transpose(v_bank[:, u, :], pairs[:, u : I // 2 : 2], identity[:])
            nc.scalar.copy(
                grouped.bitcast(F32).rearrange("m (e u) -> m e u", u=2), v_bank[:].rearrange("m u e -> m e u")
            )

        def quantise(name, grouped, tag):
            width = grouped.shape[1] // PACK
            codes = sb.tile([P, width], U32, name=name + "_codes", tag=tag, align_bytes=64)
            scales = sb.tile([P, width], U8, name=name + "_scales", align_bytes=64)
            nc.vector.quantize_mx(codes[:].bitcast(FP8X4), scales[:], grouped)
            return codes, scales

        v01_grouped = sb.tile([P, 2 * P * PACK], BF16, name="v01_grouped", tag="grouped", align_bytes=64)
        turn_values(picked0, v01_grouped[:, : P * PACK])
        turn_values(picked1, v01_grouped[:, P * PACK :])
        v01 = quantise("v01", v01_grouped[:], "val_rows2")

        w_grouped = sb.tile([P, Q, PACK], BF16, name="w_grouped", tag="grouped", align_bytes=64)
        nc.vector.tensor_tensor(
            w_grouped[:], w_bank[:].rearrange("m t q -> m q t"),
            os_sb[:].unsqueeze(1).to_broadcast([P, Q, PACK]), ALU.mult,
        )
        picked3 = placed.tile([P, I], BF16, name="picked3", offset=0, align_bytes=64)
        nc.vector.tensor_copy(picked3[:], val_rows[3][:].indirect(offsets[:]))
        w_codes, w_scales = quantise("w", w_grouped[:].rearrange("m q t -> m (q t)"), "val_rows3")

        v2_grouped = sb.tile([P, P * PACK], BF16, name="v2_grouped", align_bytes=64)
        turn_values(picked2, v2_grouped[:])
        v2 = quantise("v2", v2_grouped[:], "grouped")
        kept = sb.tile([P, E], F32, name="kept")
        nc.scalar.activation(kept[:], before_sb[:], ACT.Copy, scale=hold_sb)
        v3_grouped = sb.tile([P, P * PACK], BF16, name="v3_grouped", align_bytes=64)
        turn_values(picked3, v3_grouped[:])
        v3 = quantise("v3", v3_grouped[:], "v3_codes")

        head = (n_blocks - 1) * P
        o_head = ps.tile([P, head], F32, name="o_head")
        o_tail = ps.tile([P, P], F32, name="o_tail")
        for target, (codes, scales) in ((o_head[:, : 2 * P], v01), (o_head[:, 2 * P :], v2), (o_tail[:], v3)):
            nc.tensor.matmul_mx(
                target, lhsT=w_codes[:].bitcast(FP8X4), lhsT_scale=w_scales[:],
                rhs=codes[:].bitcast(FP8X4), rhs_scale=scales[:], start=True, stop=True,
            )
        for bank, cols in ((o_head, slice(0, head)), (o_tail, slice(head, E))):
            result = sb.tile([P, cols.stop - cols.start], F32, name="result%d" % cols.start)
            nc.vector.scalar_tensor_tensor(result[:], bank[:], new_share[:], kept[:, cols], ALU.mult, ALU.add)
            nc.sync.dma_start(out[:, cols], result[:])
